import numpy as np
import ml_dtypes


def mxq(x, axis, fmt="e4m3"):
    dtype, down = {"e4m3": (ml_dtypes.float8_e4m3fn, 7), "e5m2": (ml_dtypes.float8_e5m2, 14)}[fmt]
    v = np.moveaxis(np.asarray(x, np.float32).astype(ml_dtypes.bfloat16).astype(np.float64), axis, -1)
    blocks = v.reshape(v.shape[:-1] + (-1, 32))
    amax = np.abs(blocks).max(-1, keepdims=True)
    byte = np.maximum(np.where(amax > 0, np.frexp(amax)[1] - 1 + 127, 0) - down, 1)
    scale = np.exp2(byte - 127.0)
    codes = (blocks / scale).astype(np.float32).astype(dtype).astype(np.float64)
    return np.moveaxis((codes * scale).reshape(v.shape), -1, axis)


WIDE = False


def mx_kscale(k):
    if not WIDE:
        return np.ones(k)
    levels = np.array([10, -10, 5, -5, 0])
    if k % 512:
        return np.exp2(np.random.permutation(np.resize(levels, k // 32))).repeat(32)
    a = np.empty((k // 512, 16))
    for p in range(k // 512):
        a[p, :8] = np.random.permutation(np.resize(levels, 8))
        for g in range(8):
            far = levels[np.abs(levels - a[p, g]) >= 10]
            a[p, g + 8] = far[np.random.randint(len(far))]
    return np.exp2(a.ravel()).repeat(32)


def f64(x):
    return np.asarray(x).astype(np.float64)


def striped8(idx):
    return np.asarray(idx).reshape(8, -1, 16).transpose(0, 2, 1).reshape(128, -1).astype(np.uint16)


def unstriped8(offs):
    return offs.reshape(8, 16, -1).transpose(0, 2, 1).reshape(8, -1).astype(np.int64)


def pick8(x, idx, run):
    r = np.arange(len(x))
    return x[r[:, None], idx[r % (8 * run) // run]]


E2M1 = np.array([0.0, 0.5, 1.0, 1.5, 2.0, 3.0, 4.0, 6.0, -0.0, -0.5, -1.0, -1.5, -2.0, -3.0, -4.0, -6.0])


def pack_weight(w, fmt):
    k, n = w.shape
    w = f64(np.asarray(w, np.float32).astype(ml_dtypes.bfloat16)).reshape(k // 32, 32, n)
    amax = np.abs(w).max(1)
    if fmt == "e4m3":
        byte = np.frexp(amax)[1] - 1 + 127 - 7
    else:
        mant, ex = np.frexp(amax / 6.0)
        byte = np.where(mant > 0.5, ex, ex - 1) + 127
    byte = np.clip(np.where(amax > 0, byte, 1), 1, 254)
    scaled = (w * np.exp2(127.0 - byte)[:, None, :]).reshape(k, n).astype(np.float32)
    by_word = np.ascontiguousarray(scaled.reshape(k // 512, 128, 4, n).transpose(0, 1, 3, 2))
    if fmt == "e4m3":
        words = by_word.astype(ml_dtypes.float8_e4m3fn).view(np.uint8)
    else:
        c = by_word.astype(ml_dtypes.float4_e2m1fn).view(np.uint8) & 0xF
        words = (c[..., 0::2] | (c[..., 1::2] << 4)).reshape(k // 512, 128, 2 * n)
    return np.ascontiguousarray(words), np.ascontiguousarray(byte.astype(np.uint8).reshape(k // 512, 16, n))


def unpack_weight(words, scales, fmt):
    g, _, n = scales.shape
    words = np.ascontiguousarray(words).reshape(g, 128, n, -1)
    if fmt == "e4m3":
        vals = words.view(ml_dtypes.float8_e4m3fn).astype(np.float64)
    else:
        nib = np.empty((g, 128, n, 4), np.uint8)
        nib[..., 0::2] = words & 0xF
        nib[..., 1::2] = words >> 4
        vals = E2M1[nib]
    vals = vals * np.repeat(np.exp2(scales.astype(np.float64) - 127.0), 8, axis=1)[..., None]
    return vals.transpose(0, 1, 3, 2).reshape(g * 512, n)


D, T, Z, I, Q = 512, 1024, 1024, 512, 128


def setup_inputs():
    n = np.random.standard_normal
    idx = np.stack([np.random.permutation(T)[:I] for _ in range(8)])
    idx2 = np.stack([np.random.permutation(T)[:I] for _ in range(8)])
    idx3 = np.stack([np.random.permutation(Z)[:I] for _ in range(8)])
    idx4 = np.stack([np.random.permutation(Z)[:I] for _ in range(8)])
    fd = mx_kscale(D)
    keysp = pack_weight(n((D, T)) / fd[:, None], "e2m1")
    return {
        "query": (n((D, Q)) * 1.0 / np.sqrt(D) * fd[:, None]).astype(np.float32),
        "keys_words": keysp[0],
        "keys_scales": keysp[1],
        "old": (1.0 * n((Q, Z))).astype(np.float32),
        "offs": striped8(idx),
        "offs2": striped8(idx2),
        "offs3": striped8(idx3),
        "offs4": striped8(idx4),
    }


def reference(query, keys_words, keys_scales, old, offs, offs2, offs3, offs4):
    idx = unstriped8(offs)
    idx2 = unstriped8(offs2)
    idx3 = unstriped8(offs3)
    idx4 = unstriped8(offs4)
    keysu = unpack_weight(keys_words, keys_scales, "e2m1")
    queryq = mxq(f64(query), 0, "e4m3")
    a = queryq.T @ keysu
    ta = np.max(a, axis=1, keepdims=True)
    e1 = np.exp(pick8(a, idx, 16) - ta)
    e2 = np.exp(pick8(a, idx2, 16) - ta)
    r = e1 - e2
    f1 = np.zeros((Q, Z))
    f1[np.arange(Q)[:, None], idx3[np.arange(Q) % 128 // 16]] = r
    cc = f64(old) + f1 * 8.0
    y = pick8(cc, idx4, 16)
    return y

@@ -1,0 +1,125 @@
+from contextlib import ExitStack
+
+import concourse.mybir as mybir
+
+D, T, Z, I, Q = 512, 1024, 1024, 512, 128
+FLOPS = 2 * D * T * Q
+
+F32 = mybir.dt.float32
+BF16 = mybir.dt.bfloat16
+I32 = mybir.dt.int32
+U32 = mybir.dt.uint32
+U16 = mybir.dt.uint16
+U8 = mybir.dt.uint8
+FP8X4 = mybir.dt.float8_e4m3fn_x4
+FP4X4 = mybir.dt.float4_e2m1fn_x4
+ALU = mybir.AluOpType
+ACT = mybir.ActivationFunctionType
+
+P = 128
+PACK = 4
+GROUP = 16
+TOKENS = 256
+SLOTS = 256
+GAIN = 8.0
+
+
+def tile_attend_passedover_one_kernel(tc, query, keys_words, keys_scales, old, offs, offs2, offs3, offs4, out):
+    nc = tc.nc
+    with ExitStack() as ctx:
+        lists = ctx.enter_context(tc.tile_pool(name="lists", bufs=1))
+        work = ctx.enter_context(tc.tile_pool(name="work", bufs=1))
+        psum = ctx.enter_context(tc.psum_pool(name="psum", bufs=1))
+
+        key_scales = work.tile([P, T], U8, name="key_scales", align_bytes=64)
+        nc.vector.memset(key_scales[:].bitcast(U32), 0)
+
+        query_f32 = work.tile([P, PACK, Q], F32, name="query_f32", tag="loaded")
+        nc.sync.dma_start(out=query_f32[:], in_=query.rearrange("(p j) q -> p j q", j=PACK))
+        key_words = work.tile([P, 2 * T], U8, name="key_words", align_bytes=64)
+        nc.sync.dma_start(out=key_words[:].bitcast(I32), in_=keys_words[0].bitcast(I32))
+        for quad in range(4):
+            nc.sync.dma_start(
+                out=key_scales[32 * quad : 32 * quad + 4, :].bitcast(I32),
+                in_=keys_scales[0, 4 * quad : 4 * quad + 4, :].bitcast(I32),
+            )
+
+        def load_list(name, source):
+            held = lists.tile([P, I // GROUP], U16, name=name)
+            nc.sync.dma_start(held[:], source)
+            return held
+
+        idx2 = load_list("idx2", offs2)
+        idx1 = load_list("idx1", offs)
+        idx3 = load_list("idx3", offs3)
+        idx4 = load_list("idx4", offs4)
+
+        placed = work.tile([P, Z], F32, name="placed")
+        nc.vector.memset(placed[:], 0.0)
+
+        query_bf16 = work.tile([P, Q, PACK], BF16, name="query_bf16", align_bytes=64)
+        nc.vector.tensor_copy(out=query_bf16[:], in_=query_f32[:].rearrange("p j q -> p q j"))
+        query_words = work.tile([P, Q], U32, name="query_words", align_bytes=64)
+        query_scales = work.tile([P, Q], U8, name="query_scales", align_bytes=64)
+        nc.vector.quantize_mx(
+            out=query_words[:].bitcast(FP8X4),
+            scales=query_scales[:],
+            in_=query_bf16[:].rearrange("p q j -> p (q j)"),
+        )
+
+        old_totals = work.tile([P, Z], F32, name="old_totals", tag="loaded")
+        nc.sync.dma_start(out=old_totals[:], in_=old)
+
+        scores = work.tile([P, T], F32, name="scores")
+        part_max = work.tile([P, T // TOKENS], F32, name="part_max")
+        for c in range(T // TOKENS):
+            bank = psum.tile([P, TOKENS], F32, name=f"bank{c}")
+            nc.tensor.matmul_mx(
+                out=bank[:],
+                lhsT=query_words[:].bitcast(FP8X4),
+                lhsT_scale=query_scales[:],
+                rhs=key_words[:, 2 * c * TOKENS : 2 * (c + 1) * TOKENS].bitcast(FP4X4),
+                rhs_scale=key_scales[:, c * TOKENS : (c + 1) * TOKENS],
+                start=True,
+                stop=True,
+            )
+            nc.vector.tensor_scalar(
+                out=scores[:, c * TOKENS : (c + 1) * TOKENS],
+                in0=bank[:],
+                scalar1=1.0,
+                scalar2=None,
+                op0=ALU.mult,
+                op1=ALU.max,
+                accum_out=part_max[:, c : c + 1],
+            )
+        minus_max = work.tile([P, 1], F32, name="minus_max")
+        nc.vector.tensor_reduce(
+            out=minus_max[:], in_=part_max[:], axis=mybir.AxisListType.X, op=ALU.max, negate=True
+        )
+
+        def piece(held, s):
+            return held[:, s * SLOTS // GROUP : (s + 1) * SLOTS // GROUP]
+
+        for s in range(I // SLOTS):
+            e2 = work.tile([P, SLOTS], F32, name=f"e2_{s}")
+            nc.scalar.activation(e2[:], scores[:].indirect(piece(idx2, s)), ACT.Exp, bias=minus_max[:])
+            e1 = work.tile([P, SLOTS], F32, name=f"e1_{s}")
+            nc.scalar.activation(e1[:], scores[:].indirect(piece(idx1, s)), ACT.Exp, bias=minus_max[:])
+            minus_e2 = work.tile([P, SLOTS], F32, name=f"minus_e2_{s}")
+            if s == 0:
+                nc.vector.tensor_scalar_mul(minus_e2[:], e2[:], -1.0)
+            else:
+                nc.scalar.mul(minus_e2[:], e2[:], -1.0)
+            nc.vector.tensor_tensor(placed[:].indirect(piece(idx3, s)), e1[:], minus_e2[:], ALU.add)
+
+        totals = work.tile([P, Z], F32, name="totals")
+        nc.vector.scalar_tensor_tensor(
+            out=totals[:], in0=placed[:], scalar=GAIN, in1=old_totals[:], op0=ALU.mult, op1=ALU.add
+        )
+
+        picked0 = work.tile([P, SLOTS], F32, name="picked0")
+        nc.vector.tensor_copy(picked0[:], totals[:].indirect(piece(idx4, 0)))
+        nc.sync.dma_start(out=out[:, 0:SLOTS], in_=picked0[:])
+        picked1 = work.tile([P, SLOTS], F32, name="picked1")
+        nc.scalar.activation(picked1[:], totals[:].indirect(piece(idx4, 1)), ACT.Copy)
+        nc.scalar.dma_start(out=out[:, SLOTS:I], in_=picked1[:])

@@ -19,7 +19,7 @@ ACT = mybir.ActivationFunctionType
 P = 128
 PACK = 4
 GROUP = 16
-TOKENS = 256
+TOKENS = (128, 128, 256, 256, 256)
 SLOTS = 256
 GAIN = 8.0
 
@@ -58,7 +58,9 @@ def tile_attend_passedover_one_kernel(tc, query, keys_words, keys_scales, old, o
         nc.vector.memset(placed[:], 0.0)
 
         query_bf16 = work.tile([P, Q, PACK], BF16, name="query_bf16", align_bytes=64)
-        nc.vector.tensor_copy(out=query_bf16[:], in_=query_f32[:].rearrange("p j q -> p q j"))
+        half = Q // 2
+        nc.vector.tensor_copy(out=query_bf16[:, 0:half, :], in_=query_f32[:, :, 0:half].rearrange("p j q -> p q j"))
+        nc.scalar.copy(out=query_bf16[:, half:Q, :], in_=query_f32[:, :, half:Q].rearrange("p j q -> p q j"))
         query_words = work.tile([P, Q], U32, name="query_words", align_bytes=64)
         query_scales = work.tile([P, Q], U8, name="query_scales", align_bytes=64)
         nc.vector.quantize_mx(
@@ -71,20 +73,22 @@ def tile_attend_passedover_one_kernel(tc, query, keys_words, keys_scales, old, o
         nc.sync.dma_start(out=old_totals[:], in_=old)
 
         scores = work.tile([P, T], F32, name="scores")
-        part_max = work.tile([P, T // TOKENS], F32, name="part_max")
-        for c in range(T // TOKENS):
-            bank = psum.tile([P, TOKENS], F32, name=f"bank{c}")
+        part_max = work.tile([P, len(TOKENS)], F32, name="part_max")
+        first = 0
+        for c, width in enumerate(TOKENS):
+            last = first + width
+            bank = psum.tile([P, width], F32, name=f"bank{c}")
             nc.tensor.matmul_mx(
                 out=bank[:],
                 lhsT=query_words[:].bitcast(FP8X4),
                 lhsT_scale=query_scales[:],
-                rhs=key_words[:, 2 * c * TOKENS : 2 * (c + 1) * TOKENS].bitcast(FP4X4),
-                rhs_scale=key_scales[:, c * TOKENS : (c + 1) * TOKENS],
+                rhs=key_words[:, 2 * first : 2 * last].bitcast(FP4X4),
+                rhs_scale=key_scales[:, first:last],
                 start=True,
                 stop=True,
             )
             nc.vector.tensor_scalar(
-                out=scores[:, c * TOKENS : (c + 1) * TOKENS],
+                out=scores[:, first:last],
                 in0=bank[:],
                 scalar1=1.0,
                 scalar2=None,
@@ -92,6 +96,7 @@ def tile_attend_passedover_one_kernel(tc, query, keys_words, keys_scales, old, o
                 op1=ALU.max,
                 accum_out=part_max[:, c : c + 1],
             )
+            first = last
         minus_max = work.tile([P, 1], F32, name="minus_max")
         nc.vector.tensor_reduce(
             out=minus_max[:], in_=part_max[:], axis=mybir.AxisListType.X, op=ALU.max, negate=True

from contextlib import ExitStack

import concourse.mybir as mybir

D, T, Z, I, Q = 512, 1024, 1024, 512, 128
FLOPS = 2 * D * T * Q

F32 = mybir.dt.float32
BF16 = mybir.dt.bfloat16
I32 = mybir.dt.int32
U32 = mybir.dt.uint32
U16 = mybir.dt.uint16
U8 = mybir.dt.uint8
FP8X4 = mybir.dt.float8_e4m3fn_x4
FP4X4 = mybir.dt.float4_e2m1fn_x4
ALU = mybir.AluOpType
ACT = mybir.ActivationFunctionType

P = 128
PACK = 4
GROUP = 16
TOKENS = (128, 128, 256, 256, 256)
SLOTS = 256
GAIN = 8.0


def tile_attend_passedover_one_kernel(tc, query, keys_words, keys_scales, old, offs, offs2, offs3, offs4, out):
    nc = tc.nc
    with ExitStack() as ctx:
        lists = ctx.enter_context(tc.tile_pool(name="lists", bufs=1))
        work = ctx.enter_context(tc.tile_pool(name="work", bufs=1))
        psum = ctx.enter_context(tc.psum_pool(name="psum", bufs=1))

        key_scales = work.tile([P, T], U8, name="key_scales", align_bytes=64)
        nc.vector.memset(key_scales[:].bitcast(U32), 0)

        query_f32 = work.tile([P, PACK, Q], F32, name="query_f32", tag="loaded")
        nc.sync.dma_start(out=query_f32[:], in_=query.rearrange("(p j) q -> p j q", j=PACK))
        key_words = work.tile([P, 2 * T], U8, name="key_words", align_bytes=64)
        nc.sync.dma_start(out=key_words[:].bitcast(I32), in_=keys_words[0].bitcast(I32))
        for quad in range(4):
            nc.sync.dma_start(
                out=key_scales[32 * quad : 32 * quad + 4, :].bitcast(I32),
                in_=keys_scales[0, 4 * quad : 4 * quad + 4, :].bitcast(I32),
            )

        def load_list(name, source):
            held = lists.tile([P, I // GROUP], U16, name=name)
            nc.sync.dma_start(held[:], source)
            return held

        idx2 = load_list("idx2", offs2)
        idx1 = load_list("idx1", offs)
        idx3 = load_list("idx3", offs3)
        idx4 = load_list("idx4", offs4)

        placed = work.tile([P, Z], F32, name="placed")
        nc.vector.memset(placed[:], 0.0)

        query_bf16 = work.tile([P, Q, PACK], BF16, name="query_bf16", align_bytes=64)
        half = Q // 2
        nc.vector.tensor_copy(out=query_bf16[:, 0:half, :], in_=query_f32[:, :, 0:half].rearrange("p j q -> p q j"))
        nc.scalar.copy(out=query_bf16[:, half:Q, :], in_=query_f32[:, :, half:Q].rearrange("p j q -> p q j"))
        query_words = work.tile([P, Q], U32, name="query_words", align_bytes=64)
        query_scales = work.tile([P, Q], U8, name="query_scales", align_bytes=64)
        nc.vector.quantize_mx(
            out=query_words[:].bitcast(FP8X4),
            scales=query_scales[:],
            in_=query_bf16[:].rearrange("p q j -> p (q j)"),
        )

        old_totals = work.tile([P, Z], F32, name="old_totals", tag="loaded")
        nc.sync.dma_start(out=old_totals[:], in_=old)

        scores = work.tile([P, T], F32, name="scores")
        part_max = work.tile([P, len(TOKENS)], F32, name="part_max")
        first = 0
        for c, width in enumerate(TOKENS):
            last = first + width
            bank = psum.tile([P, width], F32, name=f"bank{c}")
            nc.tensor.matmul_mx(
                out=bank[:],
                lhsT=query_words[:].bitcast(FP8X4),
                lhsT_scale=query_scales[:],
                rhs=key_words[:, 2 * first : 2 * last].bitcast(FP4X4),
                rhs_scale=key_scales[:, first:last],
                start=True,
                stop=True,
            )
            nc.vector.tensor_scalar(
                out=scores[:, first:last],
                in0=bank[:],
                scalar1=1.0,
                scalar2=None,
                op0=ALU.mult,
                op1=ALU.max,
                accum_out=part_max[:, c : c + 1],
            )
            first = last
        minus_max = work.tile([P, 1], F32, name="minus_max")
        nc.vector.tensor_reduce(
            out=minus_max[:], in_=part_max[:], axis=mybir.AxisListType.X, op=ALU.max, negate=True
        )

        def piece(held, s):
            return held[:, s * SLOTS // GROUP : (s + 1) * SLOTS // GROUP]

        for s in range(I // SLOTS):
            e2 = work.tile([P, SLOTS], F32, name=f"e2_{s}")
            nc.scalar.activation(e2[:], scores[:].indirect(piece(idx2, s)), ACT.Exp, bias=minus_max[:])
            e1 = work.tile([P, SLOTS], F32, name=f"e1_{s}")
            nc.scalar.activation(e1[:], scores[:].indirect(piece(idx1, s)), ACT.Exp, bias=minus_max[:])
            minus_e2 = work.tile([P, SLOTS], F32, name=f"minus_e2_{s}")
            if s == 0:
                nc.vector.tensor_scalar_mul(minus_e2[:], e2[:], -1.0)
            else:
                nc.scalar.mul(minus_e2[:], e2[:], -1.0)
            nc.vector.tensor_tensor(placed[:].indirect(piece(idx3, s)), e1[:], minus_e2[:], ALU.add)

        totals = work.tile([P, Z], F32, name="totals")
        nc.vector.scalar_tensor_tensor(
            out=totals[:], in0=placed[:], scalar=GAIN, in1=old_totals[:], op0=ALU.mult, op1=ALU.add
        )

        picked0 = work.tile([P, SLOTS], F32, name="picked0")
        nc.vector.tensor_copy(picked0[:], totals[:].indirect(piece(idx4, 0)))
        nc.sync.dma_start(out=out[:, 0:SLOTS], in_=picked0[:])
        picked1 = work.tile([P, SLOTS], F32, name="picked1")
        nc.scalar.activation(picked1[:], totals[:].indirect(piece(idx4, 1)), ACT.Copy)
        nc.scalar.dma_start(out=out[:, SLOTS:I], in_=picked1[:])
